import numpy as np
import ml_dtypes


def mxq(x, axis, fmt="e4m3"):
    dtype, down = {"e4m3": (ml_dtypes.float8_e4m3fn, 7), "e5m2": (ml_dtypes.float8_e5m2, 14)}[fmt]
    v = np.moveaxis(np.asarray(x, np.float32).astype(ml_dtypes.bfloat16).astype(np.float64), axis, -1)
    blocks = v.reshape(v.shape[:-1] + (-1, 32))
    amax = np.abs(blocks).max(-1, keepdims=True)
    byte = np.maximum(np.where(amax > 0, np.frexp(amax)[1] - 1 + 127, 0) - down, 1)
    scale = np.exp2(byte - 127.0)
    codes = (blocks / scale).astype(np.float32).astype(dtype).astype(np.float64)
    return np.moveaxis((codes * scale).reshape(v.shape), -1, axis)


WIDE = False


def mx_kscale(k):
    if not WIDE:
        return np.ones(k)
    levels = np.array([10, -10, 5, -5, 0])
    if k % 512:
        return np.exp2(np.random.permutation(np.resize(levels, k // 32))).repeat(32)
    a = np.empty((k // 512, 16))
    for p in range(k // 512):
        a[p, :8] = np.random.permutation(np.resize(levels, 8))
        for g in range(8):
            far = levels[np.abs(levels - a[p, g]) >= 10]
            a[p, g + 8] = far[np.random.randint(len(far))]
    return np.exp2(a.ravel()).repeat(32)


def f64(x):
    return np.asarray(x).astype(np.float64)


def striped(idx):
    return np.tile(np.asarray(idx).reshape(-1, 16).T, (8, 1)).astype(np.uint16)


def unstriped(offs):
    return offs[:16].T.reshape(-1).astype(np.int64)


E2M1 = np.array([0.0, 0.5, 1.0, 1.5, 2.0, 3.0, 4.0, 6.0, -0.0, -0.5, -1.0, -1.5, -2.0, -3.0, -4.0, -6.0])


def pack_weight(w, fmt):
    k, n = w.shape
    w = f64(np.asarray(w, np.float32).astype(ml_dtypes.bfloat16)).reshape(k // 32, 32, n)
    amax = np.abs(w).max(1)
    if fmt == "e4m3":
        byte = np.frexp(amax)[1] - 1 + 127 - 7
    else:
        mant, ex = np.frexp(amax / 6.0)
        byte = np.where(mant > 0.5, ex, ex - 1) + 127
    byte = np.clip(np.where(amax > 0, byte, 1), 1, 254)
    scaled = (w * np.exp2(127.0 - byte)[:, None, :]).reshape(k, n).astype(np.float32)
    by_word = np.ascontiguousarray(scaled.reshape(k // 512, 128, 4, n).transpose(0, 1, 3, 2))
    if fmt == "e4m3":
        words = by_word.astype(ml_dtypes.float8_e4m3fn).view(np.uint8)
    else:
        c = by_word.astype(ml_dtypes.float4_e2m1fn).view(np.uint8) & 0xF
        words = (c[..., 0::2] | (c[..., 1::2] << 4)).reshape(k // 512, 128, 2 * n)
    return np.ascontiguousarray(words), np.ascontiguousarray(byte.astype(np.uint8).reshape(k // 512, 16, n))


def unpack_weight(words, scales, fmt):
    g, _, n = scales.shape
    words = np.ascontiguousarray(words).reshape(g, 128, n, -1)
    if fmt == "e4m3":
        vals = words.view(ml_dtypes.float8_e4m3fn).astype(np.float64)
    else:
        nib = np.empty((g, 128, n, 4), np.uint8)
        nib[..., 0::2] = words & 0xF
        nib[..., 1::2] = words >> 4
        vals = E2M1[nib]
    vals = vals * np.repeat(np.exp2(scales.astype(np.float64) - 127.0), 8, axis=1)[..., None]
    return vals.transpose(0, 1, 3, 2).reshape(g * 512, n)


def bf(x):
    return np.asarray(x, np.float32).astype(ml_dtypes.bfloat16)


def planes(Y):
    r, m = Y.shape
    b = f64(bf(Y)).reshape(r // 32, 32, m)
    amax = np.abs(b).max(1)
    byte = np.clip(np.where(amax > 0, np.frexp(amax)[1] - 1 + 127 - 7, 1), 1, 254)
    codes = (b * np.exp2(127.0 - byte)[:, None, :]).reshape(r, m).astype(np.float32).astype(ml_dtypes.float8_e4m3fn).view(np.uint8)
    words = codes.reshape(r // 512, 128, 4, m).transpose(0, 1, 3, 2)
    return np.ascontiguousarray(words), np.ascontiguousarray(byte.astype(np.uint8).reshape(r // 512, 16, m))


B, N, T, D, NQ = 1, 512, 2048, 1024, 512


def setup_inputs():
    n = np.random.standard_normal
    idx = np.random.permutation(T)[:B * N]
    s = mx_kscale(D)[:, None]
    kp = pack_weight(n((D, T)) / s, "e2m1")
    return {
        "qT": (n((B, D, NQ)) * s * (1.00 / np.sqrt(D))).astype(np.float32),
        "k_words": np.ascontiguousarray(kp[0].reshape(1, 2, 128, T, 2).transpose(0, 2, 3, 1, 4)).reshape(1, 128, T, 4),
        "k_scales": kp[1],
        "offs": striped(idx),
    }


def reference(qT, k_words, k_scales, offs):
    idx = unstriped(offs)
    pick = lambda x, which: x[:, which].reshape(x.shape[0], B, -1).transpose(1, 0, 2)
    k = unpack_weight(k_words.reshape(1, 128, T, 2, 2).transpose(0, 3, 1, 2, 4).reshape(2, 128, 2 * T), k_scales, "e2m1")
    kg = pick(k, idx)
    qq = mxq(f64(qT), 1, "e4m3")
    a = kg.transpose(0, 2, 1) @ qq
    y = np.maximum(a, 0.0)
    Y = y[0]
    words, scales = planes(Y)
    return Y, words, scales

@@ -1,0 +1,130 @@
+from contextlib import ExitStack
+
+import concourse.mybir as mybir
+
+F32 = mybir.dt.float32
+BF16 = mybir.dt.bfloat16
+I32 = mybir.dt.int32
+U32 = mybir.dt.uint32
+U16 = mybir.dt.uint16
+U8 = mybir.dt.uint8
+FP8X4 = mybir.dt.float8_e4m3fn_x4
+FP4X4 = mybir.dt.float4_e2m1fn_x4
+ACT = mybir.ActivationFunctionType
+
+P = 128
+PACK = 4
+T = 2048
+D = 1024
+NQ = 512
+SLOTS = 512
+HALF = NQ // 2
+VECTOR_COLS = [[160, 0], [256, 160]]
+WORD_PIECES = [0, 256, 512, 1024, 2048]
+FLOPS = 2 * SLOTS * D * NQ
+
+
+def interleave_views(dst, src):
+    return (dst.rearrange("p (c i) t -> p c t i", i=4), src.rearrange("p t (c i) -> p c t i", i=4))
+
+
+def tile_attend_plh_relu_topk_kernel(tc, qT, k_words, k_scales, offs, out_0, out_1, out_2):
+    nc = tc.nc
+    with ExitStack() as ctx:
+        keep = ctx.enter_context(tc.tile_pool(name="keep", bufs=1))
+        psum = ctx.enter_context(tc.psum_pool(name="psum", bufs=1))
+
+        offsets = keep.tile([P, SLOTS // 16], U16, name="offsets")
+        nc.sync.dma_start(offsets[:], offs)
+
+        word_pool = keep.tile([P, T], U32, name="word_pool", align_bytes=64)
+        scale_pool = keep.tile([P, T], U8, name="scale_pool", align_bytes=64)
+        plane1 = keep.tile([P, SLOTS], U8, name="plane1", align_bytes=64)
+        nc.vector.memset(scale_pool[:].bitcast(I32), 0)
+        nc.vector.memset(plane1[:].bitcast(I32), 0)
+
+        words_hbm = k_words[0].rearrange("p t b -> p (t b)").bitcast(I32)
+        scales_hbm = k_scales.bitcast(I32)
+        for u in range(4):
+            if u == 2:
+                for j in range(4):
+                    nc.sync.dma_start(scale_pool[j:P:16, :].bitcast(I32),
+                                      scales_hbm[:, j:16:4, :].rearrange("o g t -> g o t"))
+            tokens = slice(WORD_PIECES[u], WORD_PIECES[u + 1])
+            nc.sync.dma_start(word_pool[:, tokens].bitcast(I32), words_hbm[:, tokens])
+
+        q_rows = qT[0].rearrange("(o p t) q -> o p t q", o=2, t=PACK)
+        halves = [slice(0, HALF), slice(HALF, NQ)]
+        q_first = keep.tile([P, PACK, NQ], F32, name="q_first")
+        nc.sync.dma_start(q_first[:], q_rows[0])
+
+        plane0 = keep.tile([P, SLOTS], U8, name="plane0", align_bytes=64)
+        nc.vector.tensor_copy(plane0[:].rearrange("p (r s) -> p s r", r=PACK), scale_pool[:].indirect(offsets[:]))
+        q_second = keep.tile([P, PACK, HALF], F32, name="q_second", align_bytes=64)
+        nc.sync.dma_start(q_second[:], q_rows[1][:, :, halves[0]])
+        for j in range(4):
+            nc.scalar.dma_start(plane1[j:P:32, :].bitcast(I32), plane0[16 + j:P:32, :].bitcast(I32))
+        planes = [plane0, plane1]
+        pairs = keep.tile([P, SLOTS], U32, name="pairs", align_bytes=64)
+        nc.vector.tensor_copy(pairs[:].rearrange("p (r s) -> p s r", r=PACK), word_pool[:].indirect(offsets[:]))
+        q_late = keep.tile([P, PACK, HALF], F32, name="q_late", align_bytes=64)
+        nc.sync.dma_start(q_late[:], q_rows[1][:, :, halves[1]])
+        q_tiles = [[q_first[:, :, halves[0]], q_first[:, :, halves[1]]], [q_second[:], q_late[:]]]
+        order = [(0, 0), (0, 1), (1, 0), (1, 1)]
+        k_codes = [keep.tile([P, SLOTS], U16, name="k_codes_%d" % o, align_bytes=64) for o in range(2)]
+        pair_halves = pairs[:].bitcast(U16).rearrange("p (n o) -> p o n", o=2)
+
+        acc = [[psum.tile([P, HALF], F32, name="acc_%d_%d" % (h, r)) for r in range(PACK)] for h in range(2)]
+        y_hbm = out_0.rearrange("(s r) q -> s r q", r=PACK)
+        codes_hbm = out_1[0].rearrange("p q b -> p (q b)").bitcast(I32)
+        y_scales = keep.tile([P, NQ], U8, name="y_scales", align_bytes=64)
+
+        def multiply(o, h):
+            if h == 0:
+                nc.vector.tensor_copy(k_codes[o][:], pair_halves[:, o, :])
+            grouped = keep.tile([P, HALF, PACK], BF16, name="grouped_%d_%d" % (o, h), align_bytes=64)
+            cut = VECTOR_COLS[o][h]
+            if cut > 0:
+                dst, src = interleave_views(grouped[:, 0:cut, :], q_tiles[o][h][:, :, 0:cut])
+                nc.vector.tensor_copy(dst, src)
+            if cut < HALF:
+                dst, src = interleave_views(grouped[:, cut:HALF, :], q_tiles[o][h][:, :, cut:HALF])
+                nc.scalar.activation(dst, src, ACT.Copy)
+            codes = keep.tile([P, HALF], U32, name="q_codes_%d_%d" % (o, h), align_bytes=64)
+            scales = keep.tile([P, HALF], U8, name="q_scales_%d_%d" % (o, h), align_bytes=64)
+            nc.vector.quantize_mx(out=codes[:].bitcast(FP8X4), scales=scales[:],
+                                  in_=grouped[:].rearrange("p n t -> p (n t)"))
+            for r in range(PACK):
+                nc.tensor.matmul_mx(
+                    out=acc[h][r][:],
+                    lhsT=k_codes[o][:, r * P:(r + 1) * P].bitcast(FP4X4),
+                    lhsT_scale=planes[o][:, r * P:(r + 1) * P],
+                    rhs=codes[:].bitcast(FP8X4), rhs_scale=scales[:],
+                    start=(o == 0), stop=(o == 1))
+
+        def finish(h):
+            cols = halves[h]
+            y = keep.tile([P, PACK, HALF], F32, name="y_%d" % h)
+            for r in range(PACK):
+                if h == 1 and r % 2 == 1:
+                    nc.vector.tensor_scalar_max(y[:, r, :], acc[h][r][:], 0.0)
+                else:
+                    nc.scalar.activation(y[:, r, :], acc[h][r][:], ACT.Relu)
+            for u in range(2):
+                nc.sync.dma_start(y_hbm[:, 2 * u:2 * u + 2, cols], y[:, 2 * u:2 * u + 2, :])
+            y_grouped = keep.tile([P, HALF, PACK], BF16, name="y_grouped_%d" % h, align_bytes=64)
+            dst, src = interleave_views(y_grouped[:], y[:])
+            nc.vector.tensor_copy(dst, src)
+            y_codes = keep.tile([P, HALF], U32, name="y_codes_%d" % h, align_bytes=64)
+            nc.vector.quantize_mx(out=y_codes[:].bitcast(FP8X4), scales=y_scales[:, cols],
+                                  in_=y_grouped[:].rearrange("p n t -> p (n t)"))
+            nc.sync.dma_start(codes_hbm[:, cols], y_codes[:].bitcast(I32))
+
+        for o, h in order:
+            multiply(o, h)
+        for h in range(2):
+            finish(h)
+        scale_rows = out_2[0].bitcast(I32)
+        for g in range(4):
+            queue = nc.scalar if g % 2 else nc.sync
+            queue.dma_start(scale_rows[4 * g:4 * g + 4, :], y_scales[32 * g:32 * g + 4, :].bitcast(I32))

@@ -19,13 +19,23 @@ D = 1024
 NQ = 512
 SLOTS = 512
 HALF = NQ // 2
-VECTOR_COLS = [[160, 0], [256, 160]]
-WORD_PIECES = [0, 256, 512, 1024, 2048]
+FIRST_WORDS = 512
+VECTOR_Q_COLS = [[0, 128], [128, 160]]
+VECTOR_Y_COLS = [256, 160]
+VECTOR_RELU = [(1, 2)]
 FLOPS = 2 * SLOTS * D * NQ
 
 
-def interleave_views(dst, src):
-    return (dst.rearrange("p (c i) t -> p c t i", i=4), src.rearrange("p t (c i) -> p c t i", i=4))
+def round_and_interleave(nc, dst, src, cut):
+    for engine_cols, on_vector in ((slice(0, cut), True), (slice(cut, HALF), False)):
+        if engine_cols.start == engine_cols.stop:
+            continue
+        out = dst[:, engine_cols, :].rearrange("p (c i) t -> p c t i", i=4)
+        in_ = src[:, :, engine_cols].rearrange("p t (c i) -> p c t i", i=4)
+        if on_vector:
+            nc.vector.tensor_copy(out, in_)
+        else:
+            nc.scalar.activation(out, in_, ACT.Copy)
 
 
 def tile_attend_plh_relu_topk_kernel(tc, qT, k_words, k_scales, offs, out_0, out_1, out_2):
@@ -45,32 +55,33 @@ def tile_attend_plh_relu_topk_kernel(tc, qT, k_words, k_scales, offs, out_0, out
 
         words_hbm = k_words[0].rearrange("p t b -> p (t b)").bitcast(I32)
         scales_hbm = k_scales.bitcast(I32)
-        for u in range(4):
-            if u == 2:
-                for j in range(4):
-                    nc.sync.dma_start(scale_pool[j:P:16, :].bitcast(I32),
-                                      scales_hbm[:, j:16:4, :].rearrange("o g t -> g o t"))
-            tokens = slice(WORD_PIECES[u], WORD_PIECES[u + 1])
-            nc.sync.dma_start(word_pool[:, tokens].bitcast(I32), words_hbm[:, tokens])
+        nc.sync.dma_start(word_pool[:, 0:FIRST_WORDS].bitcast(I32), words_hbm[:, 0:FIRST_WORDS])
+        for j in range(4):
+            nc.sync.dma_start(scale_pool[j:P:16, :].bitcast(I32),
+                              scales_hbm[:, j:16:4, :].rearrange("o g t -> g o t"))
+        nc.sync.dma_start(word_pool[:, FIRST_WORDS:T].bitcast(I32), words_hbm[:, FIRST_WORDS:T])
 
         q_rows = qT[0].rearrange("(o p t) q -> o p t q", o=2, t=PACK)
         halves = [slice(0, HALF), slice(HALF, NQ)]
-        q_first = keep.tile([P, PACK, NQ], F32, name="q_first")
-        nc.sync.dma_start(q_first[:], q_rows[0])
+
+        def load_q(o, h, tag):
+            raw = keep.tile([P, PACK, HALF], F32, name="q_raw_%d_%d" % (o, h), tag=tag, align_bytes=64)
+            nc.sync.dma_start(raw[:], q_rows[o][:, :, halves[h]])
+            return raw[:]
+
+        q_raw = {}
+        q_raw[0, 0] = load_q(0, 0, "q00")
+        q_raw[1, 0] = load_q(1, 0, "q10")
 
         plane0 = keep.tile([P, SLOTS], U8, name="plane0", align_bytes=64)
         nc.vector.tensor_copy(plane0[:].rearrange("p (r s) -> p s r", r=PACK), scale_pool[:].indirect(offsets[:]))
-        q_second = keep.tile([P, PACK, HALF], F32, name="q_second", align_bytes=64)
-        nc.sync.dma_start(q_second[:], q_rows[1][:, :, halves[0]])
         for j in range(4):
-            nc.scalar.dma_start(plane1[j:P:32, :].bitcast(I32), plane0[16 + j:P:32, :].bitcast(I32))
+            nc.sync.dma_start(plane1[j:P:32, :].bitcast(I32), plane0[16 + j:P:32, :].bitcast(I32))
         planes = [plane0, plane1]
+        q_raw[0, 1] = load_q(0, 1, "q01")
+        q_raw[1, 1] = load_q(1, 1, "q11_then_y")
         pairs = keep.tile([P, SLOTS], U32, name="pairs", align_bytes=64)
         nc.vector.tensor_copy(pairs[:].rearrange("p (r s) -> p s r", r=PACK), word_pool[:].indirect(offsets[:]))
-        q_late = keep.tile([P, PACK, HALF], F32, name="q_late", align_bytes=64)
-        nc.sync.dma_start(q_late[:], q_rows[1][:, :, halves[1]])
-        q_tiles = [[q_first[:, :, halves[0]], q_first[:, :, halves[1]]], [q_second[:], q_late[:]]]
-        order = [(0, 0), (0, 1), (1, 0), (1, 1)]
         k_codes = [keep.tile([P, SLOTS], U16, name="k_codes_%d" % o, align_bytes=64) for o in range(2)]
         pair_halves = pairs[:].bitcast(U16).rearrange("p (n o) -> p o n", o=2)
 
@@ -83,13 +94,7 @@ def tile_attend_plh_relu_topk_kernel(tc, qT, k_words, k_scales, offs, out_0, out
             if h == 0:
                 nc.vector.tensor_copy(k_codes[o][:], pair_halves[:, o, :])
             grouped = keep.tile([P, HALF, PACK], BF16, name="grouped_%d_%d" % (o, h), align_bytes=64)
-            cut = VECTOR_COLS[o][h]
-            if cut > 0:
-                dst, src = interleave_views(grouped[:, 0:cut, :], q_tiles[o][h][:, :, 0:cut])
-                nc.vector.tensor_copy(dst, src)
-            if cut < HALF:
-                dst, src = interleave_views(grouped[:, cut:HALF, :], q_tiles[o][h][:, :, cut:HALF])
-                nc.scalar.activation(dst, src, ACT.Copy)
+            round_and_interleave(nc, grouped[:], q_raw[o, h], VECTOR_Q_COLS[o][h])
             codes = keep.tile([P, HALF], U32, name="q_codes_%d_%d" % (o, h), align_bytes=64)
             scales = keep.tile([P, HALF], U8, name="q_scales_%d_%d" % (o, h), align_bytes=64)
             nc.vector.quantize_mx(out=codes[:].bitcast(FP8X4), scales=scales[:],
@@ -104,24 +109,24 @@ def tile_attend_plh_relu_topk_kernel(tc, qT, k_words, k_scales, offs, out_0, out
 
         def finish(h):
             cols = halves[h]
-            y = keep.tile([P, PACK, HALF], F32, name="y_%d" % h)
+            y = keep.tile([P, PACK, HALF], F32, name="y_%d" % h, tag="q11_then_y" if h == 0 else "y_1", align_bytes=64)
             for r in range(PACK):
-                if h == 1 and r % 2 == 1:
+                if (h, r) in VECTOR_RELU:
                     nc.vector.tensor_scalar_max(y[:, r, :], acc[h][r][:], 0.0)
                 else:
                     nc.scalar.activation(y[:, r, :], acc[h][r][:], ACT.Relu)
             for u in range(2):
                 nc.sync.dma_start(y_hbm[:, 2 * u:2 * u + 2, cols], y[:, 2 * u:2 * u + 2, :])
             y_grouped = keep.tile([P, HALF, PACK], BF16, name="y_grouped_%d" % h, align_bytes=64)
-            dst, src = interleave_views(y_grouped[:], y[:])
-            nc.vector.tensor_copy(dst, src)
+            round_and_interleave(nc, y_grouped[:], y[:], VECTOR_Y_COLS[h])
             y_codes = keep.tile([P, HALF], U32, name="y_codes_%d" % h, align_bytes=64)
             nc.vector.quantize_mx(out=y_codes[:].bitcast(FP8X4), scales=y_scales[:, cols],
                                   in_=y_grouped[:].rearrange("p n t -> p (n t)"))
             nc.sync.dma_start(codes_hbm[:, cols], y_codes[:].bitcast(I32))
 
-        for o, h in order:
-            multiply(o, h)
+        for h in range(2):
+            for o in range(2):
+                multiply(o, h)
         for h in range(2):
             finish(h)
         scale_rows = out_2[0].bitcast(I32)

@@ -20,9 +20,9 @@ NQ = 512
 SLOTS = 512
 HALF = NQ // 2
 FIRST_WORDS = 512
-VECTOR_Q_COLS = [[0, 128], [128, 160]]
+VECTOR_Q_COLS = [[160, 96], [160, 256]]
 VECTOR_Y_COLS = [256, 160]
-VECTOR_RELU = [(1, 2)]
+VECTOR_RELU = [(1, 3)]
 FLOPS = 2 * SLOTS * D * NQ
 
 
@@ -70,16 +70,18 @@ def tile_attend_plh_relu_topk_kernel(tc, qT, k_words, k_scales, offs, out_0, out
             return raw[:]
 
         q_raw = {}
-        q_raw[0, 0] = load_q(0, 0, "q00")
-        q_raw[1, 0] = load_q(1, 0, "q10")
+        q_first = keep.tile([P, PACK, NQ], F32, name="q_first")
+        nc.sync.dma_start(q_first[:], q_rows[0])
+        q_raw[0, 0] = q_first[:, :, halves[0]]
+        q_raw[0, 1] = q_first[:, :, halves[1]]
 
         plane0 = keep.tile([P, SLOTS], U8, name="plane0", align_bytes=64)
         nc.vector.tensor_copy(plane0[:].rearrange("p (r s) -> p s r", r=PACK), scale_pool[:].indirect(offsets[:]))
         for j in range(4):
             nc.sync.dma_start(plane1[j:P:32, :].bitcast(I32), plane0[16 + j:P:32, :].bitcast(I32))
         planes = [plane0, plane1]
-        q_raw[0, 1] = load_q(0, 1, "q01")
-        q_raw[1, 1] = load_q(1, 1, "q11_then_y")
+        q_raw[1, 0] = load_q(1, 0, "q10")
+        q_raw[1, 1] = load_q(1, 1, "q11")
         pairs = keep.tile([P, SLOTS], U32, name="pairs", align_bytes=64)
         nc.vector.tensor_copy(pairs[:].rearrange("p (r s) -> p s r", r=PACK), word_pool[:].indirect(offsets[:]))
         k_codes = [keep.tile([P, SLOTS], U16, name="k_codes_%d" % o, align_bytes=64) for o in range(2)]
@@ -93,9 +95,9 @@ def tile_attend_plh_relu_topk_kernel(tc, qT, k_words, k_scales, offs, out_0, out
         def multiply(o, h):
             if h == 0:
                 nc.vector.tensor_copy(k_codes[o][:], pair_halves[:, o, :])
-            grouped = keep.tile([P, HALF, PACK], BF16, name="grouped_%d_%d" % (o, h), align_bytes=64)
+            grouped = keep.tile([P, HALF, PACK], BF16, name="grouped_%d_%d" % (o, h), tag="grouped_%d_%d" % (o, h), align_bytes=64)
             round_and_interleave(nc, grouped[:], q_raw[o, h], VECTOR_Q_COLS[o][h])
-            codes = keep.tile([P, HALF], U32, name="q_codes_%d_%d" % (o, h), align_bytes=64)
+            codes = keep.tile([P, HALF], U32, name="q_codes_%d_%d" % (o, h), tag="grouped_1_0" if (o, h) == (0, 1) else "codes_%d_%d" % (o, h), align_bytes=64)
             scales = keep.tile([P, HALF], U8, name="q_scales_%d_%d" % (o, h), align_bytes=64)
             nc.vector.quantize_mx(out=codes[:].bitcast(FP8X4), scales=scales[:],
                                   in_=grouped[:].rearrange("p n t -> p (n t)"))
@@ -109,7 +111,7 @@ def tile_attend_plh_relu_topk_kernel(tc, qT, k_words, k_scales, offs, out_0, out
 
         def finish(h):
             cols = halves[h]
-            y = keep.tile([P, PACK, HALF], F32, name="y_%d" % h, tag="q11_then_y" if h == 0 else "y_1", align_bytes=64)
+            y = keep.tile([P, PACK, HALF], F32, name="y_%d" % h, tag="y_%d" % h, align_bytes=64)
             for r in range(PACK):
                 if (h, r) in VECTOR_RELU:
                     nc.vector.tensor_scalar_max(y[:, r, :], acc[h][r][:], 0.0)

from contextlib import ExitStack

import concourse.mybir as mybir

F32 = mybir.dt.float32
BF16 = mybir.dt.bfloat16
I32 = mybir.dt.int32
U32 = mybir.dt.uint32
U16 = mybir.dt.uint16
U8 = mybir.dt.uint8
FP8X4 = mybir.dt.float8_e4m3fn_x4
FP4X4 = mybir.dt.float4_e2m1fn_x4
ACT = mybir.ActivationFunctionType

P = 128
PACK = 4
T = 2048
D = 1024
NQ = 512
SLOTS = 512
HALF = NQ // 2
FIRST_WORDS = 512
VECTOR_Q_COLS = [[160, 96], [160, 256]]
VECTOR_Y_COLS = [256, 160]
VECTOR_RELU = [(1, 3)]
FLOPS = 2 * SLOTS * D * NQ


def round_and_interleave(nc, dst, src, cut):
    for engine_cols, on_vector in ((slice(0, cut), True), (slice(cut, HALF), False)):
        if engine_cols.start == engine_cols.stop:
            continue
        out = dst[:, engine_cols, :].rearrange("p (c i) t -> p c t i", i=4)
        in_ = src[:, :, engine_cols].rearrange("p t (c i) -> p c t i", i=4)
        if on_vector:
            nc.vector.tensor_copy(out, in_)
        else:
            nc.scalar.activation(out, in_, ACT.Copy)


def tile_attend_plh_relu_topk_kernel(tc, qT, k_words, k_scales, offs, out_0, out_1, out_2):
    nc = tc.nc
    with ExitStack() as ctx:
        keep = ctx.enter_context(tc.tile_pool(name="keep", bufs=1))
        psum = ctx.enter_context(tc.psum_pool(name="psum", bufs=1))

        offsets = keep.tile([P, SLOTS // 16], U16, name="offsets")
        nc.sync.dma_start(offsets[:], offs)

        word_pool = keep.tile([P, T], U32, name="word_pool", align_bytes=64)
        scale_pool = keep.tile([P, T], U8, name="scale_pool", align_bytes=64)
        plane1 = keep.tile([P, SLOTS], U8, name="plane1", align_bytes=64)
        nc.vector.memset(scale_pool[:].bitcast(I32), 0)
        nc.vector.memset(plane1[:].bitcast(I32), 0)

        words_hbm = k_words[0].rearrange("p t b -> p (t b)").bitcast(I32)
        scales_hbm = k_scales.bitcast(I32)
        nc.sync.dma_start(word_pool[:, 0:FIRST_WORDS].bitcast(I32), words_hbm[:, 0:FIRST_WORDS])
        for j in range(4):
            nc.sync.dma_start(scale_pool[j:P:16, :].bitcast(I32),
                              scales_hbm[:, j:16:4, :].rearrange("o g t -> g o t"))
        nc.sync.dma_start(word_pool[:, FIRST_WORDS:T].bitcast(I32), words_hbm[:, FIRST_WORDS:T])

        q_rows = qT[0].rearrange("(o p t) q -> o p t q", o=2, t=PACK)
        halves = [slice(0, HALF), slice(HALF, NQ)]

        def load_q(o, h, tag):
            raw = keep.tile([P, PACK, HALF], F32, name="q_raw_%d_%d" % (o, h), tag=tag, align_bytes=64)
            nc.sync.dma_start(raw[:], q_rows[o][:, :, halves[h]])
            return raw[:]

        q_raw = {}
        q_first = keep.tile([P, PACK, NQ], F32, name="q_first")
        nc.sync.dma_start(q_first[:], q_rows[0])
        q_raw[0, 0] = q_first[:, :, halves[0]]
        q_raw[0, 1] = q_first[:, :, halves[1]]

        plane0 = keep.tile([P, SLOTS], U8, name="plane0", align_bytes=64)
        nc.vector.tensor_copy(plane0[:].rearrange("p (r s) -> p s r", r=PACK), scale_pool[:].indirect(offsets[:]))
        for j in range(4):
            nc.sync.dma_start(plane1[j:P:32, :].bitcast(I32), plane0[16 + j:P:32, :].bitcast(I32))
        planes = [plane0, plane1]
        q_raw[1, 0] = load_q(1, 0, "q10")
        q_raw[1, 1] = load_q(1, 1, "q11")
        pairs = keep.tile([P, SLOTS], U32, name="pairs", align_bytes=64)
        nc.vector.tensor_copy(pairs[:].rearrange("p (r s) -> p s r", r=PACK), word_pool[:].indirect(offsets[:]))
        k_codes = [keep.tile([P, SLOTS], U16, name="k_codes_%d" % o, align_bytes=64) for o in range(2)]
        pair_halves = pairs[:].bitcast(U16).rearrange("p (n o) -> p o n", o=2)

        acc = [[psum.tile([P, HALF], F32, name="acc_%d_%d" % (h, r)) for r in range(PACK)] for h in range(2)]
        y_hbm = out_0.rearrange("(s r) q -> s r q", r=PACK)
        codes_hbm = out_1[0].rearrange("p q b -> p (q b)").bitcast(I32)
        y_scales = keep.tile([P, NQ], U8, name="y_scales", align_bytes=64)

        def multiply(o, h):
            if h == 0:
                nc.vector.tensor_copy(k_codes[o][:], pair_halves[:, o, :])
            grouped = keep.tile([P, HALF, PACK], BF16, name="grouped_%d_%d" % (o, h), tag="grouped_%d_%d" % (o, h), align_bytes=64)
            round_and_interleave(nc, grouped[:], q_raw[o, h], VECTOR_Q_COLS[o][h])
            codes = keep.tile([P, HALF], U32, name="q_codes_%d_%d" % (o, h), tag="grouped_1_0" if (o, h) == (0, 1) else "codes_%d_%d" % (o, h), align_bytes=64)
            scales = keep.tile([P, HALF], U8, name="q_scales_%d_%d" % (o, h), align_bytes=64)
            nc.vector.quantize_mx(out=codes[:].bitcast(FP8X4), scales=scales[:],
                                  in_=grouped[:].rearrange("p n t -> p (n t)"))
            for r in range(PACK):
                nc.tensor.matmul_mx(
                    out=acc[h][r][:],
                    lhsT=k_codes[o][:, r * P:(r + 1) * P].bitcast(FP4X4),
                    lhsT_scale=planes[o][:, r * P:(r + 1) * P],
                    rhs=codes[:].bitcast(FP8X4), rhs_scale=scales[:],
                    start=(o == 0), stop=(o == 1))

        def finish(h):
            cols = halves[h]
            y = keep.tile([P, PACK, HALF], F32, name="y_%d" % h, tag="y_%d" % h, align_bytes=64)
            for r in range(PACK):
                if (h, r) in VECTOR_RELU:
                    nc.vector.tensor_scalar_max(y[:, r, :], acc[h][r][:], 0.0)
                else:
                    nc.scalar.activation(y[:, r, :], acc[h][r][:], ACT.Relu)
            for u in range(2):
                nc.sync.dma_start(y_hbm[:, 2 * u:2 * u + 2, cols], y[:, 2 * u:2 * u + 2, :])
            y_grouped = keep.tile([P, HALF, PACK], BF16, name="y_grouped_%d" % h, align_bytes=64)
            round_and_interleave(nc, y_grouped[:], y[:], VECTOR_Y_COLS[h])
            y_codes = keep.tile([P, HALF], U32, name="y_codes_%d" % h, align_bytes=64)
            nc.vector.quantize_mx(out=y_codes[:].bitcast(FP8X4), scales=y_scales[:, cols],
                                  in_=y_grouped[:].rearrange("p n t -> p (n t)"))
            nc.sync.dma_start(codes_hbm[:, cols], y_codes[:].bitcast(I32))

        for h in range(2):
            for o in range(2):
                multiply(o, h)
        for h in range(2):
            finish(h)
        scale_rows = out_2[0].bitcast(I32)
        for g in range(4):
            queue = nc.scalar if g % 2 else nc.sync
            queue.dma_start(scale_rows[4 * g:4 * g + 4, :], y_scales[32 * g:32 * g + 4, :].bitcast(I32))
